import numpy as np
import ml_dtypes


def mxq(x, axis, fmt="e4m3"):
    dtype, down = {"e4m3": (ml_dtypes.float8_e4m3fn, 7), "e5m2": (ml_dtypes.float8_e5m2, 14)}[fmt]
    v = np.moveaxis(np.asarray(x, np.float32).astype(ml_dtypes.bfloat16).astype(np.float64), axis, -1)
    blocks = v.reshape(v.shape[:-1] + (-1, 32))
    amax = np.abs(blocks).max(-1, keepdims=True)
    byte = np.maximum(np.where(amax > 0, np.frexp(amax)[1] - 1 + 127, 0) - down, 1)
    scale = np.exp2(byte - 127.0)
    codes = (blocks / scale).astype(np.float32).astype(dtype).astype(np.float64)
    return np.moveaxis((codes * scale).reshape(v.shape), -1, axis)


WIDE = False


def mx_kscale(k):
    if not WIDE:
        return np.ones(k)
    levels = np.array([10, -10, 5, -5, 0])
    if k % 512:
        return np.exp2(np.random.permutation(np.resize(levels, k // 32))).repeat(32)
    a = np.empty((k // 512, 16))
    for p in range(k // 512):
        a[p, :8] = np.random.permutation(np.resize(levels, 8))
        for g in range(8):
            far = levels[np.abs(levels - a[p, g]) >= 10]
            a[p, g + 8] = far[np.random.randint(len(far))]
    return np.exp2(a.ravel()).repeat(32)


def f64(x):
    return np.asarray(x).astype(np.float64)


def striped(idx):
    return np.tile(idx.reshape(-1, 16).T, (8, 1)).astype(np.uint16)


def unstriped(offs):
    return offs[:16].T.reshape(-1).astype(np.int64)


def pack_weight(w):
    k, n = w.shape
    w = f64(np.asarray(w, np.float32).astype(ml_dtypes.bfloat16)).reshape(k // 32, 32, n)
    amax = np.abs(w).max(1)
    byte = np.clip(np.where(amax > 0, np.frexp(amax)[1] - 1 + 127 - 7, 1), 1, 254)
    scaled = (w * np.exp2(127.0 - byte)[:, None, :]).reshape(k, n).astype(np.float32)
    words = np.ascontiguousarray(scaled.reshape(k // 512, 128, 4, n).transpose(0, 1, 3, 2)).astype(ml_dtypes.float8_e4m3fn).view(np.uint8)
    return words, np.ascontiguousarray(byte.astype(np.uint8).reshape(k // 512, 16, n))


def unpack_weight(words, scales):
    g, p, n, _ = words.shape
    vals = np.ascontiguousarray(words).view(ml_dtypes.float8_e4m3fn).astype(np.float64) * np.repeat(np.exp2(scales.astype(np.float64) - 127.0), 8, axis=1)[..., None]
    return vals.transpose(0, 1, 3, 2).reshape(g * 512, n)


K, T, E, C, N = 512, 2048, 16, 256, 128


def by_expert(wq, xq):
    return np.concatenate([wq[e].T @ xq[:, e * C:(e + 1) * C] for e in range(E)], axis=1)


def setup_inputs():
    n = np.random.standard_normal
    s = mx_kscale(K)[:, None]
    first = np.random.permutation(np.repeat(np.arange(E), T // E))
    second = (first + 1 + np.random.permutation(np.repeat(np.arange(E - 1), -(-T // (E - 1)))[:T])) % E
    while np.bincount(second, minlength=E).max() != T // E:
        load = np.bincount(second, minlength=E); hi, lo = int(load.argmax()), int(load.argmin())
        t = np.flatnonzero((second == hi) & (first != lo))[0]; second[t] = lo
    slot_token = np.empty(E * C, np.int64); pos = np.empty((2, T), np.int64); fill = np.zeros(E, np.int64)
    place = np.stack([np.random.permutation(C) for _ in range(E)])
    for r, deal in enumerate((first, second)):
        for t in np.random.permutation(T):
            e = deal[t]; j = e * C + place[e, fill[e]]; fill[e] += 1; slot_token[j] = t; pos[r, t] = j
    g = np.random.uniform(0.2, 0.8, T)
    packed = [pack_weight(m) for m in n((E, K, N)) / np.sqrt(K) / s[None]]
    return {
        "xT": (n((K, T)) * s).astype(np.float32),
        "w_words": np.stack([m[0] for m in packed]),
        "w_scales": np.stack([m[1] for m in packed]),
        "b": (0.3 * n((N, E))).astype(np.float32),
        "gate": np.stack([np.tile(g, (N, 1)), np.tile(1.0 - g, (N, 1))]).astype(np.float32),
        "offs": striped(slot_token),
        "pos1": striped(pos[0]),
        "pos2": striped(pos[1]),
    }


def reference(xT, w_words, w_scales, b, gate, offs, pos1, pos2):
    idx = unstriped(offs)
    xq = mxq(f64(xT)[:, idx], 0, "e4m3")
    w = np.stack([unpack_weight(w_words[e], w_scales[e]) for e in range(E)])
    y = by_expert(w, xq)
    y = y + np.repeat(f64(b), C, axis=1)
    return f64(gate[0]) * y[:, unstriped(pos1)] + f64(gate[1]) * y[:, unstriped(pos2)]

@@ -1,0 +1,178 @@
+from contextlib import ExitStack
+
+import concourse.mybir as mybir
+from concourse.masks import make_identity
+
+K, T, E, C, N = 512, 2048, 16, 256, 128
+SLOTS = E * C
+FLOPS = 2 * K * N * SLOTS
+
+F32 = mybir.dt.float32
+BF16 = mybir.dt.bfloat16
+U32 = mybir.dt.uint32
+I32 = mybir.dt.int32
+U16 = mybir.dt.uint16
+U8 = mybir.dt.uint8
+FP8X4 = mybir.dt.float8_e4m3fn_x4
+
+P = 128
+PACK = 4
+
+TOKEN_CHUNKS = (1024, 512, 384, 128)
+QUANT_MAX = {384: 256}
+WORD_CHUNKS = (1536, 1536, 1024)
+BYTE_CHUNKS = (1536, 1536, 768, 256)
+PE_ADD = 768
+PE_N = 384
+OUT_CHUNKS = (640, 384, 128, 128)
+
+
+def tile_routed_moe_kernel(tc, xT, w_words, w_scales, b, gate, offs, pos1, pos2, out):
+    nc = tc.nc
+    mult = mybir.AluOpType.mult
+    add = mybir.AluOpType.add
+    identity = mybir.ActivationFunctionType.Identity
+
+    with ExitStack() as ctx:
+        keep = ctx.enter_context(tc.tile_pool(name="keep", bufs=1))
+        comb = ctx.enter_context(tc.tile_pool(name="comb", bufs=2))
+        psum = ctx.enter_context(tc.psum_pool(name="psum", bufs=4))
+
+        offs_sb = keep.tile([P, SLOTS // 16], U16, name="offs_sb")
+        pos1_sb = keep.tile([P, T // 16], U16, name="pos1_sb")
+        pos2_sb = keep.tile([P, T // 16], U16, name="pos2_sb")
+
+        tok_codes = keep.tile([P, T], U32, name="tok_codes", align_bytes=64)
+        tok_scales = keep.tile([P, T], U8, name="tok_scales", align_bytes=64)
+        slot_codes = keep.tile([P, SLOTS], U32, name="slot_codes", align_bytes=64)
+        slot_scales = keep.tile([P, SLOTS], U8, name="slot_scales", align_bytes=64)
+        w_codes = keep.tile([P, E, N], U32, name="w_codes", align_bytes=64)
+        w_sc = keep.tile([P, E * N], U8, name="w_sc", align_bytes=64)
+        b_sb = keep.tile([P, E], F32, name="b_sb")
+        g0 = keep.tile([P, T], F32, name="g0")
+        g1 = keep.tile([P, T], F32, name="g1")
+        y = keep.tile([P, SLOTS], F32, name="y")
+        first = keep.tile([P, T], F32, name="first")
+        res = keep.tile([P, T], F32, name="res")
+
+        ident = keep.tile([P, P], F32, name="ident")
+        nc.gpsimd.memset(tok_scales[:], 0)
+        make_identity(nc, ident[:])
+        nc.vector.memset(w_sc[:].bitcast(I32), 0)
+
+        xv = xT.rearrange("(p j) t -> p j t", j=PACK)
+        raws = []
+        t0 = 0
+        for c, n in enumerate(TOKEN_CHUNKS):
+            raw = keep.tile([P, PACK, n], F32, name="raw%d" % c)
+            nc.sync.dma_start(out=raw[:], in_=xv[:, :, t0:t0 + n])
+            raws.append(raw)
+            t0 += n
+            if c == len(TOKEN_CHUNKS) - 2:
+                nc.sync.dma_start(offs_sb[:], offs)
+        nc.sync.dma_start(
+            out=w_codes[:].bitcast(I32),
+            in_=w_words.rearrange("e a p n r -> p (e a) (n r)").bitcast(I32),
+        )
+        ws_view = w_scales.rearrange("e a (q r) n -> r q (e a) n", r=4)
+        for r in range(4):
+            nc.sync.dma_start(
+                out=w_sc[r:P:32, :].bitcast(I32).rearrange("q (e n) -> q e n", e=E),
+                in_=ws_view[r].bitcast(I32),
+            )
+        nc.sync.dma_start(out=b_sb[:], in_=b)
+        nc.sync.dma_start(pos1_sb[:], pos1)
+        nc.sync.dma_start(pos2_sb[:], pos2)
+        nc.sync.dma_start(out=g0[:], in_=gate[0])
+        nc.sync.dma_start(out=g1[:], in_=gate[1])
+
+        t0 = 0
+        for c, n in enumerate(TOKEN_CHUNKS):
+            raw = raws[c]
+            grouped = keep.tile([P, n, PACK], BF16, name="grouped%d" % c, align_bytes=64)
+            nv = n if c == len(TOKEN_CHUNKS) - 1 else (5 * n) // 8
+            nc.vector.tensor_copy(
+                out=grouped[:, :nv, :].rearrange("p (c i) j -> p c j i", i=4),
+                in_=raw[:, :, :nv].rearrange("p j (c i) -> p c j i", i=4),
+            )
+            if nv < n:
+                nc.scalar.copy(
+                    out=grouped[:, nv:, :].rearrange("p (c i) j -> p c j i", i=4),
+                    in_=raw[:, :, nv:].rearrange("p j (c i) -> p c j i", i=4),
+                )
+            a = 0
+            while a < n:
+                m = min(QUANT_MAX.get(n, n), n - a)
+                nc.vector.quantize_mx(
+                    out=tok_codes[:, t0 + a:t0 + a + m].bitcast(FP8X4),
+                    scales=tok_scales[:, t0 + a:t0 + a + m],
+                    in_=grouped[:, a:a + m, :].rearrange("p t j -> p (t j)"),
+                )
+                a += m
+            t0 += n
+
+        word_ends = []
+        s0 = 0
+        for n in WORD_CHUNKS:
+            s0 += n
+            word_ends.append(s0)
+
+        def gather_words(i):
+            n = WORD_CHUNKS[i]
+            a = word_ends[i] - n
+            nc.vector.tensor_copy(
+                out=slot_codes[:, a:a + n], in_=tok_codes[:].indirect(offs_sb[:, a // 16:(a + n) // 16])
+            )
+
+        done_words = 0
+        s0 = 0
+        for n in BYTE_CHUNKS:
+            while done_words < len(WORD_CHUNKS) and word_ends[done_words] - WORD_CHUNKS[done_words] < s0 + n:
+                gather_words(done_words)
+                done_words += 1
+            nc.vector.tensor_copy(
+                out=slot_scales[:, s0:s0 + n], in_=tok_scales[:].indirect(offs_sb[:, s0 // 16:(s0 + n) // 16])
+            )
+            for e in range(s0 // C, (s0 + n) // C):
+                sl = slice(e * C, (e + 1) * C)
+                acc = psum.tile([P, C], F32, name="acc")
+                nc.tensor.matmul_mx(
+                    out=acc[:],
+                    lhsT=w_codes[:, e, :].bitcast(FP8X4),
+                    lhsT_scale=w_sc[:, e * N:(e + 1) * N],
+                    rhs=slot_codes[:, sl].bitcast(FP8X4),
+                    rhs_scale=slot_scales[:, sl],
+                    start=True,
+                    stop=True,
+                )
+                if e == E - 1:
+                    nc.vector.tensor_scalar(out=y[:, sl], in0=acc[:], scalar1=b_sb[:, e:e + 1], scalar2=None, op0=add)
+                else:
+                    nc.scalar.activation(out=y[:, sl], in_=acc[:], func=identity, bias=b_sb[:, e:e + 1], scale=1.0)
+            s0 += n
+
+        def gather_times_gate(dst, pos_sb, g, a, n):
+            nc.vector.tensor_tensor(out=dst, in0=y[:].indirect(pos_sb[:, a // 16:(a + n) // 16]), in1=g[:, a:a + n], op=mult)
+
+        gather_times_gate(first[:, 0:PE_ADD], pos1_sb, g0, 0, PE_ADD)
+        pe_second = keep.tile([P, PE_ADD], F32, name="pe_second")
+        gather_times_gate(pe_second[:], pos2_sb, g1, 0, PE_ADD)
+        for a in range(0, PE_ADD, PE_N):
+            tot = psum.tile([P, PE_N], F32, name="tot", bufs=2)
+            nc.tensor.matmul(out=tot[:], lhsT=ident[:], rhs=first[:, a:a + PE_N], start=True, stop=False)
+            nc.tensor.matmul(out=tot[:], lhsT=ident[:], rhs=pe_second[:, a:a + PE_N], start=False, stop=True)
+            nc.scalar.copy(out=res[:, a:a + PE_N], in_=tot[:])
+            nc.sync.dma_start(out=out[:, a:a + PE_N], in_=res[:, a:a + PE_N])
+        gather_times_gate(first[:, PE_ADD:T], pos1_sb, g0, PE_ADD, T - PE_ADD)
+        t0 = PE_ADD
+        pending = []
+        for n in OUT_CHUNKS:
+            second = comb.tile([P, n], F32, name="second")
+            gather_times_gate(second[:], pos2_sb, g1, t0, n)
+            pending.append((second, t0, n))
+            t0 += n
+            if len(pending) == 2 or t0 == T:
+                for s, a, m in pending:
+                    nc.vector.tensor_tensor(out=res[:, a:a + m], in0=first[:, a:a + m], in1=s[:], op=add)
+                    nc.sync.dma_start(out=out[:, a:a + m], in_=res[:, a:a + m])
+                pending = []

@@ -90,7 +90,7 @@ def tile_routed_moe_kernel(tc, xT, w_words, w_scales, b, gate, offs, pos1, pos2,
         for c, n in enumerate(TOKEN_CHUNKS):
             raw = raws[c]
             grouped = keep.tile([P, n, PACK], BF16, name="grouped%d" % c, align_bytes=64)
-            nv = n if c == len(TOKEN_CHUNKS) - 1 else (5 * n) // 8
+            nv = n if c == len(TOKEN_CHUNKS) - 1 else n // 2
             nc.vector.tensor_copy(
                 out=grouped[:, :nv, :].rearrange("p (c i) j -> p c j i", i=4),
                 in_=raw[:, :, :nv].rearrange("p j (c i) -> p c j i", i=4),

@@ -162,7 +162,7 @@ def tile_routed_moe_kernel(tc, xT, w_words, w_scales, b, gate, offs, pos1, pos2,
             nc.tensor.matmul(out=tot[:], lhsT=ident[:], rhs=first[:, a:a + PE_N], start=True, stop=False)
             nc.tensor.matmul(out=tot[:], lhsT=ident[:], rhs=pe_second[:, a:a + PE_N], start=False, stop=True)
             nc.scalar.copy(out=res[:, a:a + PE_N], in_=tot[:])
-            nc.sync.dma_start(out=out[:, a:a + PE_N], in_=res[:, a:a + PE_N])
+            nc.scalar.dma_start(out=out[:, a:a + PE_N], in_=res[:, a:a + PE_N])
         gather_times_gate(first[:, PE_ADD:T], pos1_sb, g0, PE_ADD, T - PE_ADD)
         t0 = PE_ADD
         pending = []

from contextlib import ExitStack

import concourse.mybir as mybir
from concourse.masks import make_identity

K, T, E, C, N = 512, 2048, 16, 256, 128
SLOTS = E * C
FLOPS = 2 * K * N * SLOTS

F32 = mybir.dt.float32
BF16 = mybir.dt.bfloat16
U32 = mybir.dt.uint32
I32 = mybir.dt.int32
U16 = mybir.dt.uint16
U8 = mybir.dt.uint8
FP8X4 = mybir.dt.float8_e4m3fn_x4

P = 128
PACK = 4

TOKEN_CHUNKS = (1024, 512, 384, 128)
QUANT_MAX = {384: 256}
WORD_CHUNKS = (1536, 1536, 1024)
BYTE_CHUNKS = (1536, 1536, 768, 256)
PE_ADD = 768
PE_N = 384
OUT_CHUNKS = (640, 384, 128, 128)


def tile_routed_moe_kernel(tc, xT, w_words, w_scales, b, gate, offs, pos1, pos2, out):
    nc = tc.nc
    mult = mybir.AluOpType.mult
    add = mybir.AluOpType.add
    identity = mybir.ActivationFunctionType.Identity

    with ExitStack() as ctx:
        keep = ctx.enter_context(tc.tile_pool(name="keep", bufs=1))
        comb = ctx.enter_context(tc.tile_pool(name="comb", bufs=2))
        psum = ctx.enter_context(tc.psum_pool(name="psum", bufs=4))

        offs_sb = keep.tile([P, SLOTS // 16], U16, name="offs_sb")
        pos1_sb = keep.tile([P, T // 16], U16, name="pos1_sb")
        pos2_sb = keep.tile([P, T // 16], U16, name="pos2_sb")

        tok_codes = keep.tile([P, T], U32, name="tok_codes", align_bytes=64)
        tok_scales = keep.tile([P, T], U8, name="tok_scales", align_bytes=64)
        slot_codes = keep.tile([P, SLOTS], U32, name="slot_codes", align_bytes=64)
        slot_scales = keep.tile([P, SLOTS], U8, name="slot_scales", align_bytes=64)
        w_codes = keep.tile([P, E, N], U32, name="w_codes", align_bytes=64)
        w_sc = keep.tile([P, E * N], U8, name="w_sc", align_bytes=64)
        b_sb = keep.tile([P, E], F32, name="b_sb")
        g0 = keep.tile([P, T], F32, name="g0")
        g1 = keep.tile([P, T], F32, name="g1")
        y = keep.tile([P, SLOTS], F32, name="y")
        first = keep.tile([P, T], F32, name="first")
        res = keep.tile([P, T], F32, name="res")

        ident = keep.tile([P, P], F32, name="ident")
        nc.gpsimd.memset(tok_scales[:], 0)
        make_identity(nc, ident[:])
        nc.vector.memset(w_sc[:].bitcast(I32), 0)

        xv = xT.rearrange("(p j) t -> p j t", j=PACK)
        raws = []
        t0 = 0
        for c, n in enumerate(TOKEN_CHUNKS):
            raw = keep.tile([P, PACK, n], F32, name="raw%d" % c)
            nc.sync.dma_start(out=raw[:], in_=xv[:, :, t0:t0 + n])
            raws.append(raw)
            t0 += n
            if c == len(TOKEN_CHUNKS) - 2:
                nc.sync.dma_start(offs_sb[:], offs)
        nc.sync.dma_start(
            out=w_codes[:].bitcast(I32),
            in_=w_words.rearrange("e a p n r -> p (e a) (n r)").bitcast(I32),
        )
        ws_view = w_scales.rearrange("e a (q r) n -> r q (e a) n", r=4)
        for r in range(4):
            nc.sync.dma_start(
                out=w_sc[r:P:32, :].bitcast(I32).rearrange("q (e n) -> q e n", e=E),
                in_=ws_view[r].bitcast(I32),
            )
        nc.sync.dma_start(out=b_sb[:], in_=b)
        nc.sync.dma_start(pos1_sb[:], pos1)
        nc.sync.dma_start(pos2_sb[:], pos2)
        nc.sync.dma_start(out=g0[:], in_=gate[0])
        nc.sync.dma_start(out=g1[:], in_=gate[1])

        t0 = 0
        for c, n in enumerate(TOKEN_CHUNKS):
            raw = raws[c]
            grouped = keep.tile([P, n, PACK], BF16, name="grouped%d" % c, align_bytes=64)
            nv = n if c == len(TOKEN_CHUNKS) - 1 else n // 2
            nc.vector.tensor_copy(
                out=grouped[:, :nv, :].rearrange("p (c i) j -> p c j i", i=4),
                in_=raw[:, :, :nv].rearrange("p j (c i) -> p c j i", i=4),
            )
            if nv < n:
                nc.scalar.copy(
                    out=grouped[:, nv:, :].rearrange("p (c i) j -> p c j i", i=4),
                    in_=raw[:, :, nv:].rearrange("p j (c i) -> p c j i", i=4),
                )
            a = 0
            while a < n:
                m = min(QUANT_MAX.get(n, n), n - a)
                nc.vector.quantize_mx(
                    out=tok_codes[:, t0 + a:t0 + a + m].bitcast(FP8X4),
                    scales=tok_scales[:, t0 + a:t0 + a + m],
                    in_=grouped[:, a:a + m, :].rearrange("p t j -> p (t j)"),
                )
                a += m
            t0 += n

        word_ends = []
        s0 = 0
        for n in WORD_CHUNKS:
            s0 += n
            word_ends.append(s0)

        def gather_words(i):
            n = WORD_CHUNKS[i]
            a = word_ends[i] - n
            nc.vector.tensor_copy(
                out=slot_codes[:, a:a + n], in_=tok_codes[:].indirect(offs_sb[:, a // 16:(a + n) // 16])
            )

        done_words = 0
        s0 = 0
        for n in BYTE_CHUNKS:
            while done_words < len(WORD_CHUNKS) and word_ends[done_words] - WORD_CHUNKS[done_words] < s0 + n:
                gather_words(done_words)
                done_words += 1
            nc.vector.tensor_copy(
                out=slot_scales[:, s0:s0 + n], in_=tok_scales[:].indirect(offs_sb[:, s0 // 16:(s0 + n) // 16])
            )
            for e in range(s0 // C, (s0 + n) // C):
                sl = slice(e * C, (e + 1) * C)
                acc = psum.tile([P, C], F32, name="acc")
                nc.tensor.matmul_mx(
                    out=acc[:],
                    lhsT=w_codes[:, e, :].bitcast(FP8X4),
                    lhsT_scale=w_sc[:, e * N:(e + 1) * N],
                    rhs=slot_codes[:, sl].bitcast(FP8X4),
                    rhs_scale=slot_scales[:, sl],
                    start=True,
                    stop=True,
                )
                if e == E - 1:
                    nc.vector.tensor_scalar(out=y[:, sl], in0=acc[:], scalar1=b_sb[:, e:e + 1], scalar2=None, op0=add)
                else:
                    nc.scalar.activation(out=y[:, sl], in_=acc[:], func=identity, bias=b_sb[:, e:e + 1], scale=1.0)
            s0 += n

        def gather_times_gate(dst, pos_sb, g, a, n):
            nc.vector.tensor_tensor(out=dst, in0=y[:].indirect(pos_sb[:, a // 16:(a + n) // 16]), in1=g[:, a:a + n], op=mult)

        gather_times_gate(first[:, 0:PE_ADD], pos1_sb, g0, 0, PE_ADD)
        pe_second = keep.tile([P, PE_ADD], F32, name="pe_second")
        gather_times_gate(pe_second[:], pos2_sb, g1, 0, PE_ADD)
        for a in range(0, PE_ADD, PE_N):
            tot = psum.tile([P, PE_N], F32, name="tot", bufs=2)
            nc.tensor.matmul(out=tot[:], lhsT=ident[:], rhs=first[:, a:a + PE_N], start=True, stop=False)
            nc.tensor.matmul(out=tot[:], lhsT=ident[:], rhs=pe_second[:, a:a + PE_N], start=False, stop=True)
            nc.scalar.copy(out=res[:, a:a + PE_N], in_=tot[:])
            nc.scalar.dma_start(out=out[:, a:a + PE_N], in_=res[:, a:a + PE_N])
        gather_times_gate(first[:, PE_ADD:T], pos1_sb, g0, PE_ADD, T - PE_ADD)
        t0 = PE_ADD
        pending = []
        for n in OUT_CHUNKS:
            second = comb.tile([P, n], F32, name="second")
            gather_times_gate(second[:], pos2_sb, g1, t0, n)
            pending.append((second, t0, n))
            t0 += n
            if len(pending) == 2 or t0 == T:
                for s, a, m in pending:
                    nc.vector.tensor_tensor(out=res[:, a:a + m], in0=first[:, a:a + m], in1=s[:], op=add)
                    nc.sync.dma_start(out=out[:, a:a + m], in_=res[:, a:a + m])
                pending = []
